import numpy as np
import ml_dtypes


def mxq(x, axis, fmt="e4m3"):
    dtype, down = {"e4m3": (ml_dtypes.float8_e4m3fn, 7), "e5m2": (ml_dtypes.float8_e5m2, 14)}[fmt]
    v = np.moveaxis(np.asarray(x, np.float32).astype(ml_dtypes.bfloat16).astype(np.float64), axis, -1)
    blocks = v.reshape(v.shape[:-1] + (-1, 32))
    amax = np.abs(blocks).max(-1, keepdims=True)
    byte = np.maximum(np.where(amax > 0, np.frexp(amax)[1] - 1 + 127, 0) - down, 1)
    scale = np.exp2(byte - 127.0)
    codes = (blocks / scale).astype(np.float32).astype(dtype).astype(np.float64)
    return np.moveaxis((codes * scale).reshape(v.shape), -1, axis)


WIDE = False


def mx_kscale(k):
    if not WIDE:
        return np.ones(k)
    levels = np.array([10, -10, 5, -5, 0])
    if k % 512:
        return np.exp2(np.random.permutation(np.resize(levels, k // 32))).repeat(32)
    a = np.empty((k // 512, 16))
    for p in range(k // 512):
        a[p, :8] = np.random.permutation(np.resize(levels, 8))
        for g in range(8):
            far = levels[np.abs(levels - a[p, g]) >= 10]
            a[p, g + 8] = far[np.random.randint(len(far))]
    return np.exp2(a.ravel()).repeat(32)


def f64(x):
    return np.asarray(x).astype(np.float64)


def striped(idx):
    return np.tile(idx.reshape(-1, 16).T, (8, 1)).astype(np.uint16)


def unstriped(offs):
    return offs[:16].T.reshape(-1).astype(np.int64)


def striped8(idx):
    return np.concatenate([x.reshape(-1, 16).T for x in idx]).astype(np.uint16)


def runs(offs, k):
    lists = np.stack([offs[16 * r : 16 * r + 16].T.reshape(-1) for r in range(8)]).astype(np.int64)
    return lists[np.arange(k) % 512 // 64]


def pack_weight(w):
    k, n = w.shape
    w = f64(np.asarray(w, np.float32).astype(ml_dtypes.bfloat16)).reshape(k // 32, 32, n)
    amax = np.abs(w).max(1)
    byte = np.clip(np.where(amax > 0, np.frexp(amax)[1] - 1 + 127 - 7, 1), 1, 254)
    scaled = (w * np.exp2(127.0 - byte)[:, None, :]).reshape(k, n).astype(np.float32)
    words = np.ascontiguousarray(scaled.reshape(k // 512, 128, 4, n).transpose(0, 1, 3, 2)).astype(ml_dtypes.float8_e4m3fn).view(np.uint8)
    return words, np.ascontiguousarray(byte.astype(np.uint8).reshape(k // 512, 16, n))


def unpack_weight(words, scales):
    g, p, n, _ = words.shape
    vals = np.ascontiguousarray(words).view(ml_dtypes.float8_e4m3fn).astype(np.float64) * np.repeat(np.exp2(scales.astype(np.float64) - 127.0), 8, axis=1)[..., None]
    return vals.transpose(0, 1, 3, 2).reshape(g * 512, n)


def sigmoid(v):
    return 1.0 / (1.0 + np.exp(-np.maximum(v, -700.0)))


K, T, S, N, G, H, U = 512, 1024, 256, 512, 2048, 512, 512


def setup_inputs():
    n = np.random.standard_normal
    s = mx_kscale(K)[:, None]
    u = mx_kscale(K)
    packed_xT = pack_weight(n((K, T)) * s)
    packed_dT = pack_weight(n((K, G)) / s)
    packed_w1 = pack_weight(n((H, N)) / np.sqrt(2 * H) / u[:, None])
    packed_w2 = pack_weight(n((K, N)) / np.sqrt(2 * K) / s)
    perm = np.random.permutation(U)
    return {
        "x_words": packed_xT[0],
        "x_scales": packed_xT[1],
        "d_words": packed_dT[0],
        "d_scales": packed_dT[1],
        "gn": (np.random.uniform(0.5, 1.5, (H, 1)) * u[:, None]).astype(np.float32),
        "w1_words": packed_w1[0],
        "w1_scales": packed_w1[1],
        "w2_words": packed_w2[0],
        "w2_scales": packed_w2[1],
        "sl": np.random.uniform(1.0, 2.0, (N, 1)).astype(np.float32),
        "th": (0.5 * n((N, 1))).astype(np.float32),
        "offs": striped8(np.random.randint(0, T, (8, S))),
        "k1": striped8(np.random.randint(0, G, (8, H))),
        "hz": striped8(np.random.randint(0, T, (8, S))),
        "k2": striped8(np.random.randint(0, G, (8, H))),
        "hy": striped8(np.random.randint(0, T, (8, S))),
        "n1": striped(perm[:S]),
        "n2": striped(perm[S:]),
        "n3": striped(np.random.permutation(S)),
    }


def reference(x_words, x_scales, d_words, d_scales, gn, w1_words, w1_scales, w2_words, w2_scales, sl, th, offs, k1, hz, k2, hy, n1, n2, n3):
    d_k1 = unpack_weight(d_words, d_scales)[np.arange(K)[:, None], runs(k1, K)]
    xq = unpack_weight(x_words, x_scales)[np.arange(K)[:, None], runs(offs, K)]
    d_k2 = unpack_weight(d_words, d_scales)[np.arange(K)[:, None], runs(k2, K)]
    x_hz = unpack_weight(x_words, x_scales)[np.arange(K)[:, None], runs(hz, K)]
    h = 0.0625 * (d_k1.T @ xq + d_k2.T @ x_hz)
    z = f64(gn) * h
    x_hy = unpack_weight(x_words, x_scales)[np.arange(K)[:, None], runs(hy, K)]
    h2 = unpack_weight(w1_words, w1_scales).T @ mxq(z, 0, "e4m3") + unpack_weight(w2_words, w2_scales).T @ x_hy
    sg = sigmoid(f64(sl) * (h2[:, unstriped(n3)] - f64(th)))
    st = h2 * sg
    ph = np.zeros((N, U))
    ph[:, unstriped(n1)] = h2
    out = ph.copy()
    out[:, unstriped(n2)] = st
    return out

@@ -1,0 +1,233 @@
+from contextlib import ExitStack
+
+import concourse.mybir as mybir
+from concourse.masks import make_identity
+
+K, T, S, N, G, H, U = 512, 1024, 256, 512, 2048, 512, 512
+FLOPS = 2 * (2 * K * H * S + H * N * S + K * N * S)
+
+F32 = mybir.dt.float32
+BF16 = mybir.dt.bfloat16
+I32 = mybir.dt.int32
+U32 = mybir.dt.uint32
+U16 = mybir.dt.uint16
+U8 = mybir.dt.uint8
+FP8X4 = mybir.dt.float8_e4m3fn_x4
+ACT = mybir.ActivationFunctionType
+MULT = mybir.AluOpType.mult
+ADD = mybir.AluOpType.add
+
+P = 128
+PACK = 4
+HALF = S // 2
+BLOCKS = N // P
+
+
+def tile_picked_mhhonhepag_none_p_kernel(
+    tc, x_words, x_scales, d_words, d_scales, gn, w1_words, w1_scales, w2_words, w2_scales,
+    sl, th, offs, k1, hz, k2, hy, n1, n2, n3, out
+):
+    nc = tc.nc
+    with ExitStack() as ctx:
+        lists = ctx.enter_context(tc.tile_pool(name="lists", bufs=1))
+        keep = ctx.enter_context(tc.tile_pool(name="keep", bufs=1))
+        ps_h = ctx.enter_context(tc.psum_pool(name="ps_h", bufs=2))
+        ps_o = ctx.enter_context(tc.psum_pool(name="ps_o", bufs=4))
+
+        def sb(shape, dtype, name, tag=""):
+            return keep.tile(shape, dtype, name=name, tag=tag or name, align_bytes=64)
+
+        def load_list(src, name):
+            t = lists.tile(list(src.shape), U16, name=name)
+            nc.sync.dma_start(t[:], src)
+            return t
+
+        def load_scale_table(src, width, name):
+            t = sb([P, width], U8, name)
+            rows = src[0].bitcast(I32)
+            nc.sync.dma_start(t[:].bitcast(I32), rows.unsqueeze(1).to_broadcast([16, 8, width // 4]))
+            return t
+
+        def load_words(src, width, name):
+            t = sb([P, width], U32, name)
+            nc.sync.dma_start(t[:].bitcast(I32), src[0].rearrange("p n t -> p (n t)").bitcast(I32))
+            return t
+
+        def entries(lst, half):
+            return lst[:, half * HALF // 16 : (half + 1) * HALF // 16]
+
+        l_offs = load_list(offs, "l_offs")
+        xs_tab = load_scale_table(x_scales, T, "xs_tab")
+        l_hz = load_list(hz, "l_hz")
+        l_hy = load_list(hy, "l_hy")
+        ds_tab = load_scale_table(d_scales, G, "ds_tab")
+        l_k1 = load_list(k1, "l_k1")
+        l_k2 = load_list(k2, "l_k2")
+        xw_tab = load_words(x_words, T, "xw_tab")
+        dw_tab = load_words(d_words, G, "dw_tab")
+        x_lists = (l_offs, l_hz, l_hy)
+        d_lists = (l_k1, l_k2)
+
+        gn4 = sb([P, PACK], F32, "gn4")
+        nc.scalar.dma_start(gn4[:], gn.rearrange("(p t) o -> p (t o)", t=PACK))
+        rows = sb([P, P], F32, "rows")
+        nc.vector.memset(rows[:], 0.0)
+        nc.scalar.dma_start(rows[0:BLOCKS, :], sl.rearrange("(a p) o -> a (p o)", p=P))
+        nc.scalar.dma_start(rows[BLOCKS : 2 * BLOCKS, :], th.rearrange("(a p) o -> a (p o)", p=P))
+        l_n1 = load_list(n1, "l_n1")
+        l_n3 = load_list(n3, "l_n3")
+        l_n2 = load_list(n2, "l_n2")
+        w2w = load_words(w2_words, N, "w2w")
+        w1w = load_words(w1_words, N, "w1w")
+
+        ident = sb([P, P], F32, "ident")
+        make_identity(nc, ident[:])
+        turned = ps_h.tile([P, P], F32, name="turned", tag="hb")
+        nc.tensor.transpose(turned[:], rows[:], ident[:])
+        slth = sb([P, 2 * BLOCKS], F32, "slth")
+        nc.scalar.copy(slth[:], turned[:, 0 : 2 * BLOCKS])
+        prod = sb([P, BLOCKS], F32, "prod")
+        bias = sb([P, BLOCKS], F32, "bias")
+        nc.gpsimd.tensor_tensor(prod[:], slth[:, 0:BLOCKS], slth[:, BLOCKS : 2 * BLOCKS], MULT)
+        nc.gpsimd.tensor_scalar(bias[:], prod[:], -1.0, 0.0, MULT, ADD)
+
+        XS = 3 * HALF
+        planes = [sb([P, XS + 2 * H], U8, "plane0"), sb([P, XS], U8, "plane1")]
+        for plane in planes:
+            nc.vector.memset(plane[:].bitcast(I32), 0)
+
+        def place_rows(plane, got):
+            for j in range(4):
+                nc.scalar.dma_start(plane[j:P:32, :].bitcast(I32), got[8 * j : P : 32, :].bitcast(I32))
+
+        def gather_x_scales(got, half):
+            for i, lst in enumerate(x_lists):
+                nc.vector.tensor_copy(got[:, i * HALF : (i + 1) * HALF], xs_tab[:].indirect(entries(lst, half)))
+
+        got0 = sb([P, XS + 2 * H], U8, "got0")
+        gather_x_scales(got0, 0)
+        for i, lst in enumerate(d_lists):
+            nc.vector.tensor_copy(got0[:, XS + i * H : XS + (i + 1) * H], ds_tab[:].indirect(lst[:]))
+        place_rows(planes[0], got0)
+
+        ws = sb([P, 2 * N], U8, "ws", tag="ds_tab")
+        nc.gpsimd.memset(ws[:].bitcast(I32), 0)
+        for i, src in enumerate((w2_scales, w1_scales)):
+            for q in range(4):
+                nc.sync.dma_start(
+                    ws[32 * q : 32 * q + 4, i * N : (i + 1) * N].bitcast(I32),
+                    src[0, 4 * q : 4 * q + 4, :].bitcast(I32),
+                )
+
+        def gather_x_words(dst, i, half):
+            nc.vector.tensor_copy(dst, xw_tab[:].indirect(entries(x_lists[i], half)))
+            return dst
+
+        xw0 = [gather_x_words(sb([P, HALF], U32, "xw0_%d" % i)[:], i, 0) for i in range(2)]
+
+        dw_got = []
+        for i, lst in enumerate(d_lists):
+            got = sb([P, H], U32, "dw_got%d" % i)
+            nc.vector.tensor_copy(got[:], dw_tab[:].indirect(lst[:]))
+            dw_got.append(got)
+
+        def deal(dst, src):
+            nc.vector.tensor_copy(
+                dst.rearrange("p (s t m) -> p s m t", t=PACK, m=P),
+                src.rearrange("p (s m t) -> p s m t", t=PACK, m=P),
+            )
+
+        dw_dealt = [sb([P, H], U32, "dw_dealt%d" % i) for i in range(2)]
+        ds_dealt = sb([P, 2 * H], U8, "ds_dealt")
+        deal(dw_dealt[0][:], dw_got[0][:])
+        deal(ds_dealt[:], planes[0][:, XS:])
+        deal(dw_dealt[1][:], dw_got[1][:])
+
+        got1 = sb([P, XS], U8, "got1", tag="dw_got1")
+        gather_x_scales(got1, 1)
+        place_rows(planes[1], got1)
+        xw0.append(gather_x_words(sb([P, HALF], U32, "xw0_2", tag="dw_got0")[:], 2, 0))
+
+        h2 = [sb([P, S], F32, "h2_%d" % a) for a in range(BLOCKS)]
+        page = [sb([P, U], F32, "page%d" % a) for a in range(BLOCKS)]
+
+        def first_layer(half, xw):
+            hb = ps_h.tile([P, PACK, HALF], F32, name="hb", tag="hb")
+            for i in range(2):
+                for t in range(PACK):
+                    nc.tensor.matmul_mx(
+                        out=hb[:, t, :],
+                        lhsT=dw_dealt[i][:, t * P : (t + 1) * P].bitcast(FP8X4),
+                        lhsT_scale=ds_dealt[:, i * H + t * P : i * H + (t + 1) * P],
+                        rhs=xw[i].bitcast(FP8X4),
+                        rhs_scale=planes[half][:, i * HALF : (i + 1) * HALF],
+                        start=(i == 0 and t == 0),
+                        stop=(i == 1 and t == PACK - 1),
+                    )
+            z = sb([P, HALF, PACK], BF16, "z%d" % half)
+            nc.vector.scalar_tensor_tensor(
+                z[:],
+                hb[:].rearrange("p t j -> p j t"),
+                0.0625,
+                gn4[:].unsqueeze(1).to_broadcast([P, HALF, PACK]),
+                MULT,
+                MULT,
+            )
+            zw = sb([P, HALF], U32, "zw%d" % half)
+            zs = sb([P, HALF], U8, "zs%d" % half)
+            nc.vector.quantize_mx(zw[:].bitcast(FP8X4), zs[:], z[:].rearrange("p j t -> p (j t)"))
+            return zw, zs
+
+        def second_layer(half, xw_hy, zw, zs):
+            cols = slice(half * HALF, (half + 1) * HALF)
+            for a in range(BLOCKS):
+                ob = ps_o.tile([P, HALF], F32, name="ob")
+                nc.tensor.matmul_mx(
+                    out=ob[:],
+                    lhsT=w2w[:, a * P : (a + 1) * P].bitcast(FP8X4),
+                    lhsT_scale=ws[:, a * P : (a + 1) * P],
+                    rhs=xw_hy.bitcast(FP8X4),
+                    rhs_scale=planes[half][:, 2 * HALF : 3 * HALF],
+                    start=True,
+                    stop=False,
+                )
+                nc.tensor.matmul_mx(
+                    out=ob[:],
+                    lhsT=w1w[:, a * P : (a + 1) * P].bitcast(FP8X4),
+                    lhsT_scale=ws[:, N + a * P : N + (a + 1) * P],
+                    rhs=zw[:].bitcast(FP8X4),
+                    rhs_scale=zs[:],
+                    start=False,
+                    stop=True,
+                )
+                nc.vector.tensor_copy(h2[a][:, cols], ob[:])
+
+        def put_h2(a, half):
+            cols = slice(half * HALF, (half + 1) * HALF)
+            nc.scalar.activation(page[a][:].indirect(entries(l_n1, half)), h2[a][:, cols], ACT.Copy)
+
+        zw, zs = first_layer(0, xw0)
+        xw1_hy = gather_x_words(sb([P, HALF], U32, "xw1_2", tag="xw0_1")[:], 2, 1)
+        second_layer(0, xw0[2], zw, zs)
+        for a in range(BLOCKS):
+            put_h2(a, 0)
+        xw1_pair = sb([P, 2, HALF], U32, "xw1_pair", tag="z0")
+        xw1 = [gather_x_words(xw1_pair[:, i, :], i, 1) for i in range(2)]
+        zw, zs = first_layer(1, xw1)
+        second_layer(1, xw1_hy, zw, zs)
+
+        for a in range(BLOCKS):
+            sg = sb([P, S], F32, "sg%d" % a)
+            for half in range(2):
+                nc.scalar.activation(
+                    sg[:, half * HALF : (half + 1) * HALF],
+                    h2[a][:].indirect(entries(l_n3, half)),
+                    ACT.Sigmoid,
+                    bias=bias[:, a : a + 1],
+                    scale=slth[:, a : a + 1],
+                )
+            st = sb([P, S], F32, "st%d" % a)
+            nc.vector.tensor_tensor(st[:], h2[a][:], sg[:], MULT)
+            put_h2(a, 1)
+            nc.scalar.activation(page[a][:].indirect(l_n2[:]), st[:], ACT.Copy)
+            nc.sync.dma_start(out[a * P : (a + 1) * P, :], page[a][:])

@@ -80,6 +80,11 @@ def tile_picked_mhhonhepag_none_p_kernel(
         w2w = load_words(w2_words, N, "w2w")
         w1w = load_words(w1_words, N, "w1w")
 
+        warm_in = sb([P, 1], F32, "warm_in")
+        warm_out = sb([P, 1], F32, "warm_out")
+        nc.vector.memset(warm_in[:], 0.0)
+        nc.scalar.activation(warm_out[:], warm_in[:], ACT.Sigmoid)
+
         ident = sb([P, P], F32, "ident")
         make_identity(nc, ident[:])
         turned = ps_h.tile([P, P], F32, name="turned", tag="hb")

@@ -15,7 +15,6 @@ U8 = mybir.dt.uint8
 FP8X4 = mybir.dt.float8_e4m3fn_x4
 ACT = mybir.ActivationFunctionType
 MULT = mybir.AluOpType.mult
-ADD = mybir.AluOpType.add
 
 P = 128
 PACK = 4
@@ -31,8 +30,7 @@ def tile_picked_mhhonhepag_none_p_kernel(
     with ExitStack() as ctx:
         lists = ctx.enter_context(tc.tile_pool(name="lists", bufs=1))
         keep = ctx.enter_context(tc.tile_pool(name="keep", bufs=1))
-        ps_h = ctx.enter_context(tc.psum_pool(name="ps_h", bufs=2))
-        ps_o = ctx.enter_context(tc.psum_pool(name="ps_o", bufs=4))
+        psum = ctx.enter_context(tc.psum_pool(name="psum", bufs=1))
 
         def sb(shape, dtype, name, tag=""):
             return keep.tile(shape, dtype, name=name, tag=tag or name, align_bytes=64)
@@ -63,38 +61,53 @@ def tile_picked_mhhonhepag_none_p_kernel(
         ds_tab = load_scale_table(d_scales, G, "ds_tab")
         l_k1 = load_list(k1, "l_k1")
         l_k2 = load_list(k2, "l_k2")
-        xw_tab = load_words(x_words, T, "xw_tab")
         dw_tab = load_words(d_words, G, "dw_tab")
+        xw_tab = load_words(x_words, T, "xw_tab")
         x_lists = (l_offs, l_hz, l_hy)
         d_lists = (l_k1, l_k2)
 
+        ws = sb([P, 2 * N], U8, "ws")
+        nc.vector.memset(ws[:].bitcast(I32), 0)
+
+        def load_weight_scales(queue, i, src, q):
+            queue.dma_start(
+                ws[32 * q : 32 * q + 4, i * N : (i + 1) * N].bitcast(I32),
+                src[0, 4 * q : 4 * q + 4, :].bitcast(I32),
+            )
+
+        ident = sb([P, P], F32, "ident")
+        make_identity(nc, ident[:])
+        for q in range(4):
+            load_weight_scales(nc.gpsimd, 1, w1_scales, q)
+        for q in range(2):
+            load_weight_scales(nc.gpsimd, 0, w2_scales, q)
+
         gn4 = sb([P, PACK], F32, "gn4")
-        nc.scalar.dma_start(gn4[:], gn.rearrange("(p t) o -> p (t o)", t=PACK))
+        nc.sync.dma_start(gn4[:], gn.rearrange("(p t) o -> p (t o)", t=PACK))
         rows = sb([P, P], F32, "rows")
         nc.vector.memset(rows[:], 0.0)
-        nc.scalar.dma_start(rows[0:BLOCKS, :], sl.rearrange("(a p) o -> a (p o)", p=P))
-        nc.scalar.dma_start(rows[BLOCKS : 2 * BLOCKS, :], th.rearrange("(a p) o -> a (p o)", p=P))
+        nc.sync.dma_start(rows[0:BLOCKS, :], sl.rearrange("(a p) o -> a (p o)", p=P))
+        nc.sync.dma_start(rows[BLOCKS : 2 * BLOCKS, :], th.rearrange("(a p) o -> a (p o)", p=P))
         l_n1 = load_list(n1, "l_n1")
         l_n3 = load_list(n3, "l_n3")
         l_n2 = load_list(n2, "l_n2")
-        w2w = load_words(w2_words, N, "w2w")
-        w1w = load_words(w1_words, N, "w1w")
 
         warm_in = sb([P, 1], F32, "warm_in")
         warm_out = sb([P, 1], F32, "warm_out")
         nc.vector.memset(warm_in[:], 0.0)
         nc.scalar.activation(warm_out[:], warm_in[:], ACT.Sigmoid)
 
-        ident = sb([P, P], F32, "ident")
-        make_identity(nc, ident[:])
-        turned = ps_h.tile([P, P], F32, name="turned", tag="hb")
+        turned = psum.tile([P, P], F32, name="turned")
         nc.tensor.transpose(turned[:], rows[:], ident[:])
         slth = sb([P, 2 * BLOCKS], F32, "slth")
         nc.scalar.copy(slth[:], turned[:, 0 : 2 * BLOCKS])
-        prod = sb([P, BLOCKS], F32, "prod")
+        neg_sl = sb([P, BLOCKS], F32, "neg_sl")
+        nc.scalar.activation(neg_sl[:], turned[:, 0:BLOCKS], ACT.Copy, scale=-1.0)
         bias = sb([P, BLOCKS], F32, "bias")
-        nc.gpsimd.tensor_tensor(prod[:], slth[:, 0:BLOCKS], slth[:, BLOCKS : 2 * BLOCKS], MULT)
-        nc.gpsimd.tensor_scalar(bias[:], prod[:], -1.0, 0.0, MULT, ADD)
+        for a in range(BLOCKS):
+            nc.scalar.activation(
+                bias[:, a : a + 1], slth[:, BLOCKS + a : BLOCKS + a + 1], ACT.Copy, scale=neg_sl[:, a : a + 1]
+            )
 
         XS = 3 * HALF
         planes = [sb([P, XS + 2 * H], U8, "plane0"), sb([P, XS], U8, "plane1")]
@@ -103,26 +116,30 @@ def tile_picked_mhhonhepag_none_p_kernel(
 
         def place_rows(plane, got):
             for j in range(4):
-                nc.scalar.dma_start(plane[j:P:32, :].bitcast(I32), got[8 * j : P : 32, :].bitcast(I32))
+                nc.sync.dma_start(plane[j:P:32, :].bitcast(I32), got[8 * j : P : 32, :].bitcast(I32))
 
-        def gather_x_scales(got, half):
-            for i, lst in enumerate(x_lists):
-                nc.vector.tensor_copy(got[:, i * HALF : (i + 1) * HALF], xs_tab[:].indirect(entries(lst, half)))
+        def gather_x_scales(got, i, half):
+            nc.vector.tensor_copy(got[:, i * HALF : (i + 1) * HALF], xs_tab[:].indirect(entries(x_lists[i], half)))
+
+        def deal(dst, src):
+            nc.vector.tensor_copy(
+                dst.rearrange("p (s t m) -> p s m t", t=PACK, m=P),
+                src.rearrange("p (s m t) -> p s m t", t=PACK, m=P),
+            )
 
         got0 = sb([P, XS + 2 * H], U8, "got0")
-        gather_x_scales(got0, 0)
+        for i in range(3):
+            gather_x_scales(got0, i, 0)
         for i, lst in enumerate(d_lists):
             nc.vector.tensor_copy(got0[:, XS + i * H : XS + (i + 1) * H], ds_tab[:].indirect(lst[:]))
-        place_rows(planes[0], got0)
-
-        ws = sb([P, 2 * N], U8, "ws", tag="ds_tab")
-        nc.gpsimd.memset(ws[:].bitcast(I32), 0)
-        for i, src in enumerate((w2_scales, w1_scales)):
-            for q in range(4):
-                nc.sync.dma_start(
-                    ws[32 * q : 32 * q + 4, i * N : (i + 1) * N].bitcast(I32),
-                    src[0, 4 * q : 4 * q + 4, :].bitcast(I32),
-                )
+        dealt0 = sb([P, XS + 2 * H], U8, "dealt0")
+        nc.vector.tensor_copy(dealt0[:, 0:XS].bitcast(I32), got0[:, 0:XS].bitcast(I32))
+        deal(dealt0[:, XS:], got0[:, XS:])
+        place_rows(planes[0], dealt0)
+        for q in range(2, 4):
+            load_weight_scales(nc.sync, 0, w2_scales, q)
+        w2w = load_words(w2_words, N, "w2w")
+        w1w = load_words(w1_words, N, "w1w")
 
         def gather_x_words(dst, i, half):
             nc.vector.tensor_copy(dst, xw_tab[:].indirect(entries(x_lists[i], half)))
@@ -136,20 +153,13 @@ def tile_picked_mhhonhepag_none_p_kernel(
             nc.vector.tensor_copy(got[:], dw_tab[:].indirect(lst[:]))
             dw_got.append(got)
 
-        def deal(dst, src):
-            nc.vector.tensor_copy(
-                dst.rearrange("p (s t m) -> p s m t", t=PACK, m=P),
-                src.rearrange("p (s m t) -> p s m t", t=PACK, m=P),
-            )
-
         dw_dealt = [sb([P, H], U32, "dw_dealt%d" % i) for i in range(2)]
-        ds_dealt = sb([P, 2 * H], U8, "ds_dealt")
         deal(dw_dealt[0][:], dw_got[0][:])
-        deal(ds_dealt[:], planes[0][:, XS:])
         deal(dw_dealt[1][:], dw_got[1][:])
 
         got1 = sb([P, XS], U8, "got1", tag="dw_got1")
-        gather_x_scales(got1, 1)
+        for i in range(3):
+            gather_x_scales(got1, i, 1)
         place_rows(planes[1], got1)
         xw0.append(gather_x_words(sb([P, HALF], U32, "xw0_2", tag="dw_got0")[:], 2, 0))
 
@@ -157,13 +167,13 @@ def tile_picked_mhhonhepag_none_p_kernel(
         page = [sb([P, U], F32, "page%d" % a) for a in range(BLOCKS)]
 
         def first_layer(half, xw):
-            hb = ps_h.tile([P, PACK, HALF], F32, name="hb", tag="hb")
+            hb = psum.tile([P, PACK, HALF], F32, name="hb", tag=("hb", "ob0")[half])
             for i in range(2):
                 for t in range(PACK):
                     nc.tensor.matmul_mx(
                         out=hb[:, t, :],
                         lhsT=dw_dealt[i][:, t * P : (t + 1) * P].bitcast(FP8X4),
-                        lhsT_scale=ds_dealt[:, i * H + t * P : i * H + (t + 1) * P],
+                        lhsT_scale=planes[0][:, XS + i * H + t * P : XS + i * H + (t + 1) * P],
                         rhs=xw[i].bitcast(FP8X4),
                         rhs_scale=planes[half][:, i * HALF : (i + 1) * HALF],
                         start=(i == 0 and t == 0),
@@ -186,7 +196,7 @@ def tile_picked_mhhonhepag_none_p_kernel(
         def second_layer(half, xw_hy, zw, zs):
             cols = slice(half * HALF, (half + 1) * HALF)
             for a in range(BLOCKS):
-                ob = ps_o.tile([P, HALF], F32, name="ob")
+                ob = psum.tile([P, HALF], F32, name="ob", tag="ob%d" % a)
                 nc.tensor.matmul_mx(
                     out=ob[:],
                     lhsT=w2w[:, a * P : (a + 1) * P].bitcast(FP8X4),

@@ -77,10 +77,6 @@ def tile_picked_mhhonhepag_none_p_kernel(
 
         ident = sb([P, P], F32, "ident")
         make_identity(nc, ident[:])
-        for q in range(4):
-            load_weight_scales(nc.gpsimd, 1, w1_scales, q)
-        for q in range(2):
-            load_weight_scales(nc.gpsimd, 0, w2_scales, q)
 
         gn4 = sb([P, PACK], F32, "gn4")
         nc.sync.dma_start(gn4[:], gn.rearrange("(p t) o -> p (t o)", t=PACK))
@@ -136,10 +132,11 @@ def tile_picked_mhhonhepag_none_p_kernel(
         nc.vector.tensor_copy(dealt0[:, 0:XS].bitcast(I32), got0[:, 0:XS].bitcast(I32))
         deal(dealt0[:, XS:], got0[:, XS:])
         place_rows(planes[0], dealt0)
-        for q in range(2, 4):
-            load_weight_scales(nc.sync, 0, w2_scales, q)
         w2w = load_words(w2_words, N, "w2w")
         w1w = load_words(w1_words, N, "w1w")
+        for i, src in enumerate((w2_scales, w1_scales)):
+            for q in range(4):
+                load_weight_scales(nc.sync, i, src, q)
 
         def gather_x_words(dst, i, half):
             nc.vector.tensor_copy(dst, xw_tab[:].indirect(entries(x_lists[i], half)))
@@ -163,7 +160,9 @@ def tile_picked_mhhonhepag_none_p_kernel(
         place_rows(planes[1], got1)
         xw0.append(gather_x_words(sb([P, HALF], U32, "xw0_2", tag="dw_got0")[:], 2, 0))
 
-        h2 = [sb([P, S], F32, "h2_%d" % a) for a in range(BLOCKS)]
+        h2 = [sb([P, 2 * S], F32, "h2_%d" % a) for a in range(BLOCKS)]
+        for a in range(BLOCKS):
+            nc.gpsimd.memset(h2[a][:, S:], 0.0)
         page = [sb([P, U], F32, "page%d" % a) for a in range(BLOCKS)]
 
         def first_layer(half, xw):
@@ -180,17 +179,22 @@ def tile_picked_mhhonhepag_none_p_kernel(
                         stop=(i == 1 and t == PACK - 1),
                     )
             z = sb([P, HALF, PACK], BF16, "z%d" % half)
-            nc.vector.scalar_tensor_tensor(
-                z[:],
-                hb[:].rearrange("p t j -> p j t"),
-                0.0625,
-                gn4[:].unsqueeze(1).to_broadcast([P, HALF, PACK]),
-                MULT,
-                MULT,
-            )
             zw = sb([P, HALF], U32, "zw%d" % half)
             zs = sb([P, HALF], U8, "zs%d" % half)
-            nc.vector.quantize_mx(zw[:].bitcast(FP8X4), zs[:], z[:].rearrange("p j t -> p (j t)"))
+            parts = [slice(c * HALF // 2, (c + 1) * HALF // 2) for c in range(2)]
+            for cols in parts:
+                nc.vector.scalar_tensor_tensor(
+                    z[:, cols, :],
+                    hb[:, :, cols].rearrange("p t j -> p j t"),
+                    0.0625,
+                    gn4[:].unsqueeze(1).to_broadcast([P, HALF // 2, PACK]),
+                    MULT,
+                    MULT,
+                )
+            for cols in parts:
+                nc.vector.quantize_mx(
+                    zw[:, cols].bitcast(FP8X4), zs[:, cols], z[:, cols, :].rearrange("p j t -> p (j t)")
+                )
             return zw, zs
 
         def second_layer(half, xw_hy, zw, zs):
@@ -222,27 +226,26 @@ def tile_picked_mhhonhepag_none_p_kernel(
             nc.scalar.activation(page[a][:].indirect(entries(l_n1, half)), h2[a][:, cols], ACT.Copy)
 
         zw, zs = first_layer(0, xw0)
-        xw1_hy = gather_x_words(sb([P, HALF], U32, "xw1_2", tag="xw0_1")[:], 2, 1)
         second_layer(0, xw0[2], zw, zs)
         for a in range(BLOCKS):
             put_h2(a, 0)
         xw1_pair = sb([P, 2, HALF], U32, "xw1_pair", tag="z0")
         xw1 = [gather_x_words(xw1_pair[:, i, :], i, 1) for i in range(2)]
+        xw1_hy = gather_x_words(sb([P, HALF], U32, "xw1_2", tag="zw0")[:], 2, 1)
         zw, zs = first_layer(1, xw1)
         second_layer(1, xw1_hy, zw, zs)
 
         for a in range(BLOCKS):
             sg = sb([P, S], F32, "sg%d" % a)
-            for half in range(2):
-                nc.scalar.activation(
-                    sg[:, half * HALF : (half + 1) * HALF],
-                    h2[a][:].indirect(entries(l_n3, half)),
-                    ACT.Sigmoid,
-                    bias=bias[:, a : a + 1],
-                    scale=slth[:, a : a + 1],
-                )
+            nc.scalar.activation(
+                sg[:],
+                h2[a][:].indirect(l_n3[:]),
+                ACT.Sigmoid,
+                bias=bias[:, a : a + 1],
+                scale=slth[:, a : a + 1],
+            )
             st = sb([P, S], F32, "st%d" % a)
-            nc.vector.tensor_tensor(st[:], h2[a][:], sg[:], MULT)
+            nc.vector.tensor_tensor(st[:], h2[a][:, 0:S], sg[:], MULT)
             put_h2(a, 1)
             nc.scalar.activation(page[a][:].indirect(l_n2[:]), st[:], ACT.Copy)
             nc.sync.dma_start(out[a * P : (a + 1) * P, :], page[a][:])

from contextlib import ExitStack

import concourse.mybir as mybir
from concourse.masks import make_identity

K, T, S, N, G, H, U = 512, 1024, 256, 512, 2048, 512, 512
FLOPS = 2 * (2 * K * H * S + H * N * S + K * N * S)

F32 = mybir.dt.float32
BF16 = mybir.dt.bfloat16
I32 = mybir.dt.int32
U32 = mybir.dt.uint32
U16 = mybir.dt.uint16
U8 = mybir.dt.uint8
FP8X4 = mybir.dt.float8_e4m3fn_x4
ACT = mybir.ActivationFunctionType
MULT = mybir.AluOpType.mult

P = 128
PACK = 4
HALF = S // 2
BLOCKS = N // P


def tile_picked_mhhonhepag_none_p_kernel(
    tc, x_words, x_scales, d_words, d_scales, gn, w1_words, w1_scales, w2_words, w2_scales,
    sl, th, offs, k1, hz, k2, hy, n1, n2, n3, out
):
    nc = tc.nc
    with ExitStack() as ctx:
        lists = ctx.enter_context(tc.tile_pool(name="lists", bufs=1))
        keep = ctx.enter_context(tc.tile_pool(name="keep", bufs=1))
        psum = ctx.enter_context(tc.psum_pool(name="psum", bufs=1))

        def sb(shape, dtype, name, tag=""):
            return keep.tile(shape, dtype, name=name, tag=tag or name, align_bytes=64)

        def load_list(src, name):
            t = lists.tile(list(src.shape), U16, name=name)
            nc.sync.dma_start(t[:], src)
            return t

        def load_scale_table(src, width, name):
            t = sb([P, width], U8, name)
            rows = src[0].bitcast(I32)
            nc.sync.dma_start(t[:].bitcast(I32), rows.unsqueeze(1).to_broadcast([16, 8, width // 4]))
            return t

        def load_words(src, width, name):
            t = sb([P, width], U32, name)
            nc.sync.dma_start(t[:].bitcast(I32), src[0].rearrange("p n t -> p (n t)").bitcast(I32))
            return t

        def entries(lst, half):
            return lst[:, half * HALF // 16 : (half + 1) * HALF // 16]

        l_offs = load_list(offs, "l_offs")
        xs_tab = load_scale_table(x_scales, T, "xs_tab")
        l_hz = load_list(hz, "l_hz")
        l_hy = load_list(hy, "l_hy")
        ds_tab = load_scale_table(d_scales, G, "ds_tab")
        l_k1 = load_list(k1, "l_k1")
        l_k2 = load_list(k2, "l_k2")
        dw_tab = load_words(d_words, G, "dw_tab")
        xw_tab = load_words(x_words, T, "xw_tab")
        x_lists = (l_offs, l_hz, l_hy)
        d_lists = (l_k1, l_k2)

        ws = sb([P, 2 * N], U8, "ws")
        nc.vector.memset(ws[:].bitcast(I32), 0)

        def load_weight_scales(queue, i, src, q):
            queue.dma_start(
                ws[32 * q : 32 * q + 4, i * N : (i + 1) * N].bitcast(I32),
                src[0, 4 * q : 4 * q + 4, :].bitcast(I32),
            )

        ident = sb([P, P], F32, "ident")
        make_identity(nc, ident[:])

        gn4 = sb([P, PACK], F32, "gn4")
        nc.sync.dma_start(gn4[:], gn.rearrange("(p t) o -> p (t o)", t=PACK))
        rows = sb([P, P], F32, "rows")
        nc.vector.memset(rows[:], 0.0)
        nc.sync.dma_start(rows[0:BLOCKS, :], sl.rearrange("(a p) o -> a (p o)", p=P))
        nc.sync.dma_start(rows[BLOCKS : 2 * BLOCKS, :], th.rearrange("(a p) o -> a (p o)", p=P))
        l_n1 = load_list(n1, "l_n1")
        l_n3 = load_list(n3, "l_n3")
        l_n2 = load_list(n2, "l_n2")

        warm_in = sb([P, 1], F32, "warm_in")
        warm_out = sb([P, 1], F32, "warm_out")
        nc.vector.memset(warm_in[:], 0.0)
        nc.scalar.activation(warm_out[:], warm_in[:], ACT.Sigmoid)

        turned = psum.tile([P, P], F32, name="turned")
        nc.tensor.transpose(turned[:], rows[:], ident[:])
        slth = sb([P, 2 * BLOCKS], F32, "slth")
        nc.scalar.copy(slth[:], turned[:, 0 : 2 * BLOCKS])
        neg_sl = sb([P, BLOCKS], F32, "neg_sl")
        nc.scalar.activation(neg_sl[:], turned[:, 0:BLOCKS], ACT.Copy, scale=-1.0)
        bias = sb([P, BLOCKS], F32, "bias")
        for a in range(BLOCKS):
            nc.scalar.activation(
                bias[:, a : a + 1], slth[:, BLOCKS + a : BLOCKS + a + 1], ACT.Copy, scale=neg_sl[:, a : a + 1]
            )

        XS = 3 * HALF
        planes = [sb([P, XS + 2 * H], U8, "plane0"), sb([P, XS], U8, "plane1")]
        for plane in planes:
            nc.vector.memset(plane[:].bitcast(I32), 0)

        def place_rows(plane, got):
            for j in range(4):
                nc.sync.dma_start(plane[j:P:32, :].bitcast(I32), got[8 * j : P : 32, :].bitcast(I32))

        def gather_x_scales(got, i, half):
            nc.vector.tensor_copy(got[:, i * HALF : (i + 1) * HALF], xs_tab[:].indirect(entries(x_lists[i], half)))

        def deal(dst, src):
            nc.vector.tensor_copy(
                dst.rearrange("p (s t m) -> p s m t", t=PACK, m=P),
                src.rearrange("p (s m t) -> p s m t", t=PACK, m=P),
            )

        got0 = sb([P, XS + 2 * H], U8, "got0")
        for i in range(3):
            gather_x_scales(got0, i, 0)
        for i, lst in enumerate(d_lists):
            nc.vector.tensor_copy(got0[:, XS + i * H : XS + (i + 1) * H], ds_tab[:].indirect(lst[:]))
        dealt0 = sb([P, XS + 2 * H], U8, "dealt0")
        nc.vector.tensor_copy(dealt0[:, 0:XS].bitcast(I32), got0[:, 0:XS].bitcast(I32))
        deal(dealt0[:, XS:], got0[:, XS:])
        place_rows(planes[0], dealt0)
        w2w = load_words(w2_words, N, "w2w")
        w1w = load_words(w1_words, N, "w1w")
        for i, src in enumerate((w2_scales, w1_scales)):
            for q in range(4):
                load_weight_scales(nc.sync, i, src, q)

        def gather_x_words(dst, i, half):
            nc.vector.tensor_copy(dst, xw_tab[:].indirect(entries(x_lists[i], half)))
            return dst

        xw0 = [gather_x_words(sb([P, HALF], U32, "xw0_%d" % i)[:], i, 0) for i in range(2)]

        dw_got = []
        for i, lst in enumerate(d_lists):
            got = sb([P, H], U32, "dw_got%d" % i)
            nc.vector.tensor_copy(got[:], dw_tab[:].indirect(lst[:]))
            dw_got.append(got)

        dw_dealt = [sb([P, H], U32, "dw_dealt%d" % i) for i in range(2)]
        deal(dw_dealt[0][:], dw_got[0][:])
        deal(dw_dealt[1][:], dw_got[1][:])

        got1 = sb([P, XS], U8, "got1", tag="dw_got1")
        for i in range(3):
            gather_x_scales(got1, i, 1)
        place_rows(planes[1], got1)
        xw0.append(gather_x_words(sb([P, HALF], U32, "xw0_2", tag="dw_got0")[:], 2, 0))

        h2 = [sb([P, 2 * S], F32, "h2_%d" % a) for a in range(BLOCKS)]
        for a in range(BLOCKS):
            nc.gpsimd.memset(h2[a][:, S:], 0.0)
        page = [sb([P, U], F32, "page%d" % a) for a in range(BLOCKS)]

        def first_layer(half, xw):
            hb = psum.tile([P, PACK, HALF], F32, name="hb", tag=("hb", "ob0")[half])
            for i in range(2):
                for t in range(PACK):
                    nc.tensor.matmul_mx(
                        out=hb[:, t, :],
                        lhsT=dw_dealt[i][:, t * P : (t + 1) * P].bitcast(FP8X4),
                        lhsT_scale=planes[0][:, XS + i * H + t * P : XS + i * H + (t + 1) * P],
                        rhs=xw[i].bitcast(FP8X4),
                        rhs_scale=planes[half][:, i * HALF : (i + 1) * HALF],
                        start=(i == 0 and t == 0),
                        stop=(i == 1 and t == PACK - 1),
                    )
            z = sb([P, HALF, PACK], BF16, "z%d" % half)
            zw = sb([P, HALF], U32, "zw%d" % half)
            zs = sb([P, HALF], U8, "zs%d" % half)
            parts = [slice(c * HALF // 2, (c + 1) * HALF // 2) for c in range(2)]
            for cols in parts:
                nc.vector.scalar_tensor_tensor(
                    z[:, cols, :],
                    hb[:, :, cols].rearrange("p t j -> p j t"),
                    0.0625,
                    gn4[:].unsqueeze(1).to_broadcast([P, HALF // 2, PACK]),
                    MULT,
                    MULT,
                )
            for cols in parts:
                nc.vector.quantize_mx(
                    zw[:, cols].bitcast(FP8X4), zs[:, cols], z[:, cols, :].rearrange("p j t -> p (j t)")
                )
            return zw, zs

        def second_layer(half, xw_hy, zw, zs):
            cols = slice(half * HALF, (half + 1) * HALF)
            for a in range(BLOCKS):
                ob = psum.tile([P, HALF], F32, name="ob", tag="ob%d" % a)
                nc.tensor.matmul_mx(
                    out=ob[:],
                    lhsT=w2w[:, a * P : (a + 1) * P].bitcast(FP8X4),
                    lhsT_scale=ws[:, a * P : (a + 1) * P],
                    rhs=xw_hy.bitcast(FP8X4),
                    rhs_scale=planes[half][:, 2 * HALF : 3 * HALF],
                    start=True,
                    stop=False,
                )
                nc.tensor.matmul_mx(
                    out=ob[:],
                    lhsT=w1w[:, a * P : (a + 1) * P].bitcast(FP8X4),
                    lhsT_scale=ws[:, N + a * P : N + (a + 1) * P],
                    rhs=zw[:].bitcast(FP8X4),
                    rhs_scale=zs[:],
                    start=False,
                    stop=True,
                )
                nc.vector.tensor_copy(h2[a][:, cols], ob[:])

        def put_h2(a, half):
            cols = slice(half * HALF, (half + 1) * HALF)
            nc.scalar.activation(page[a][:].indirect(entries(l_n1, half)), h2[a][:, cols], ACT.Copy)

        zw, zs = first_layer(0, xw0)
        second_layer(0, xw0[2], zw, zs)
        for a in range(BLOCKS):
            put_h2(a, 0)
        xw1_pair = sb([P, 2, HALF], U32, "xw1_pair", tag="z0")
        xw1 = [gather_x_words(xw1_pair[:, i, :], i, 1) for i in range(2)]
        xw1_hy = gather_x_words(sb([P, HALF], U32, "xw1_2", tag="zw0")[:], 2, 1)
        zw, zs = first_layer(1, xw1)
        second_layer(1, xw1_hy, zw, zs)

        for a in range(BLOCKS):
            sg = sb([P, S], F32, "sg%d" % a)
            nc.scalar.activation(
                sg[:],
                h2[a][:].indirect(l_n3[:]),
                ACT.Sigmoid,
                bias=bias[:, a : a + 1],
                scale=slth[:, a : a + 1],
            )
            st = sb([P, S], F32, "st%d" % a)
            nc.vector.tensor_tensor(st[:], h2[a][:, 0:S], sg[:], MULT)
            put_h2(a, 1)
            nc.scalar.activation(page[a][:].indirect(l_n2[:]), st[:], ACT.Copy)
            nc.sync.dma_start(out[a * P : (a + 1) * P, :], page[a][:])
